import numpy as np
import ml_dtypes


def mxq(x, axis, fmt="e4m3"):
    dtype, down = {"e4m3": (ml_dtypes.float8_e4m3fn, 7), "e5m2": (ml_dtypes.float8_e5m2, 14)}[fmt]
    v = np.moveaxis(np.asarray(x, np.float32).astype(ml_dtypes.bfloat16).astype(np.float64), axis, -1)
    blocks = v.reshape(v.shape[:-1] + (-1, 32))
    amax = np.abs(blocks).max(-1, keepdims=True)
    byte = np.maximum(np.where(amax > 0, np.frexp(amax)[1] - 1 + 127, 0) - down, 1)
    scale = np.exp2(byte - 127.0)
    codes = (blocks / scale).astype(np.float32).astype(dtype).astype(np.float64)
    return np.moveaxis((codes * scale).reshape(v.shape), -1, axis)


WIDE = False


def mx_kscale(k):
    if not WIDE:
        return np.ones(k)
    levels = np.array([24, -24, 12, -12, 0])
    if k % 512:
        return np.exp2(np.random.permutation(np.resize(levels, k // 32))).repeat(32)
    a = np.empty((k // 512, 16))
    for p in range(k // 512):
        a[p, :8] = np.random.permutation(np.resize(levels, 8))
        for g in range(8):
            far = levels[np.abs(levels - a[p, g]) >= 10]
            a[p, g + 8] = far[np.random.randint(len(far))]
    return np.exp2(a.ravel()).repeat(32)


def f64(x):
    return np.asarray(x).astype(np.float64)


def striped8(idx):
    return np.concatenate([v.reshape(-1, 16).T for v in idx]).astype(np.uint16)


def unstriped8(offs):
    return np.stack([offs[16 * g:16 * g + 16].T.reshape(-1) for g in range(8)]).astype(np.int64)


E2M1 = np.array([0.0, 0.5, 1.0, 1.5, 2.0, 3.0, 4.0, 6.0, -0.0, -0.5, -1.0, -1.5, -2.0, -3.0, -4.0, -6.0])


def pack_weight(w, fmt):
    k, n = w.shape
    w = f64(np.asarray(w, np.float32).astype(ml_dtypes.bfloat16)).reshape(k // 32, 32, n)
    amax = np.abs(w).max(1)
    if fmt == "e4m3":
        byte = np.frexp(amax)[1] - 1 + 127 - 7
    else:
        mant, ex = np.frexp(amax / 6.0)
        byte = np.where(mant > 0.5, ex, ex - 1) + 127
    byte = np.clip(np.where(amax > 0, byte, 1), 1, 254)
    scaled = (w * np.exp2(127.0 - byte)[:, None, :]).reshape(k, n).astype(np.float32)
    by_word = np.ascontiguousarray(scaled.reshape(k // 512, 128, 4, n).transpose(0, 1, 3, 2))
    if fmt == "e4m3":
        words = by_word.astype(ml_dtypes.float8_e4m3fn).view(np.uint8)
    else:
        c = by_word.astype(ml_dtypes.float4_e2m1fn).view(np.uint8) & 0xF
        words = (c[..., 0::2] | (c[..., 1::2] << 4)).reshape(k // 512, 128, 2 * n)
    return np.ascontiguousarray(words), np.ascontiguousarray(byte.astype(np.uint8).reshape(k // 512, 16, n))


def unpack_weight(words, scales, fmt):
    g, _, n = scales.shape
    words = np.ascontiguousarray(words).reshape(g, 128, n, -1)
    if fmt == "e4m3":
        vals = words.view(ml_dtypes.float8_e4m3fn).astype(np.float64)
    else:
        nib = np.empty((g, 128, n, 4), np.uint8)
        nib[..., 0::2] = words & 0xF
        nib[..., 1::2] = words >> 4
        vals = E2M1[nib]
    vals = vals * np.repeat(np.exp2(scales.astype(np.float64) - 127.0), 8, axis=1)[..., None]
    return vals.transpose(0, 1, 3, 2).reshape(g * 512, n)


def planes(y):
    n, m = y.shape
    v = y.astype(np.float32).astype(ml_dtypes.bfloat16).astype(np.float64).reshape(n // 32, 32, m)
    top = np.abs(v).max(1)
    byte = np.clip(np.where(top > 0, np.frexp(top)[1] - 1 + 127 - 7, 1), 1, 254)
    codes = (v * np.exp2(127.0 - byte)[:, None, :]).reshape(n, m).astype(np.float32).astype(ml_dtypes.float8_e4m3fn).view(np.uint8)
    words = codes.reshape(n // 512, 128, 4, m).transpose(0, 1, 3, 2)
    return np.ascontiguousarray(words), np.ascontiguousarray(byte.astype(np.uint8).reshape(n // 512, 16, m))


K, L, N, T, J = 512, 512, 512, 2048, 1024


def setup_inputs():
    n = np.random.standard_normal
    s = mx_kscale(K)[:, None]
    s2 = mx_kscale(L)[:, None]
    p_wa = pack_weight(n((K, N)) / np.sqrt(K) / s, "e4m3")
    p_wb = pack_weight(n((L, N)) / np.sqrt(L) / s2, "e4m3")
    return {
        "xT": (n((K, T)) * s).astype(np.float32),
        "wgt": np.repeat(np.random.uniform(0.5, 2.0, (8, J)), 16, axis=0).astype(np.float32),
        "zT": (n((L, T)) * s2).astype(np.float32),
        "wgt2": np.repeat(np.random.uniform(0.5, 2.0, (8, J)), 16, axis=0).astype(np.float32),
        "wa_words": p_wa[0],
        "wa_scales": p_wa[1],
        "wb_words": p_wb[0],
        "wb_scales": p_wb[1],
        "offs": striped8(np.stack([np.random.permutation(T)[:J] for _ in range(8)])),
        "offs2": striped8(np.stack([np.random.permutation(T)[:J] for _ in range(8)])),
    }


def reference(xT, wgt, zT, wgt2, wa_words, wa_scales, wb_words, wb_scales, offs, offs2):
    idx = unstriped8(offs)
    idx2 = unstriped8(offs2)
    rows = np.arange(K)
    xg = f64(wgt)[rows // 4 % 128] * f64(xT)[rows[:, None], idx[rows % 512 // 64]]
    xT_ = mxq(xg, 0, "e4m3")
    rows = np.arange(L)
    xg = f64(wgt2)[rows // 4 % 128] * f64(zT)[rows[:, None], idx2[rows % 512 // 64]]
    zT_ = mxq(xg, 0, "e4m3")
    wa_ = unpack_weight(wa_words, wa_scales, "e4m3")
    wb_ = unpack_weight(wb_words, wb_scales, "e4m3")
    ya = wa_.T @ xT_
    yb = wb_.T @ zT_
    out_0 = ya * yb
    return (out_0,) + planes(out_0)

@@ -1,0 +1,178 @@
+from contextlib import ExitStack
+
+import concourse.mybir as mybir
+
+K, L, N, T, J = 512, 512, 512, 2048, 1024
+FLOPS = 2 * (K + L) * N * J
+
+F32 = mybir.dt.float32
+BF16 = mybir.dt.bfloat16
+I32 = mybir.dt.int32
+U16 = mybir.dt.uint16
+U8 = mybir.dt.uint8
+FP8X4 = mybir.dt.float8_e4m3fn_x4
+MULT = mybir.AluOpType.mult
+
+P = 128
+PACK = 4
+BLOCK = 128
+QUARTER = 256
+
+
+def tile_list_mul_noneP_kernel(
+    tc, xT, wgt, zT, wgt2, wa_words, wa_scales, wb_words, wb_scales, offs, offs2, out_0, out_1, out_2
+):
+    nc = tc.nc
+    with ExitStack() as ctx:
+        keep = ctx.enter_context(tc.tile_pool(name="keep", bufs=1))
+        psum = ctx.enter_context(tc.psum_pool(name="psum", bufs=8))
+
+        lists = [keep.tile([P, J // 16], U16, name="list%d" % s) for s in range(2)]
+        gains = [keep.tile([P, J], F32, name="gain%d" % s) for s in range(2)]
+        planes = [[keep.tile([P, T], F32, name="plane%d_%d" % (s, i)) for i in range(PACK)] for s in range(2)]
+        picked = [keep.tile([P, PACK, J], F32, name="picked%d" % s) for s in range(2)]
+        woven = [keep.tile([P, J, PACK], BF16, name="woven%d" % s, align_bytes=64) for s in range(2)]
+        act_words = [keep.tile([P, J], I32, name="act_words%d" % s, align_bytes=64) for s in range(2)]
+        act_scales = [keep.tile([P, J], U8, name="act_scales%d" % s, align_bytes=64) for s in range(2)]
+        w_raw = [keep.tile([P, N], I32, name="w_raw%d" % s) for s in range(2)]
+        w_words = [keep.tile([P, PACK, P], I32, name="w_words%d" % s, align_bytes=64) for s in range(2)]
+        ws_raw = keep.tile([P, N], U8, name="ws_raw")
+        w_scales = keep.tile([P, PACK, P], U8, name="w_scales", align_bytes=64)
+        ya = keep.tile([P, J // BLOCK, PACK, BLOCK], F32, name="ya")
+        y = keep.tile([P, PACK, J], F32, name="y")
+        y_woven = keep.tile([P, J, PACK], BF16, name="y_woven", align_bytes=64)
+        y_words = keep.tile([P, J], I32, name="y_words", align_bytes=64)
+        y_scales = keep.tile([P, J], U8, name="y_scales", align_bytes=64)
+
+        sources = [xT, zT]
+        scale_sources = [wa_scales, wb_scales]
+        word_sources = [wa_words, wb_words]
+
+        def load_plane(s, i):
+            nc.sync.dma_start(out=planes[s][i][:], in_=sources[s].rearrange("(p i) t -> p i t", i=PACK)[:, i, :])
+
+        def load_scale_rows(s, q):
+            nc.sync.dma_start(
+                out=ws_raw[32 * q + 4 * s : 32 * q + 4 * s + 4, :].bitcast(I32),
+                in_=scale_sources[s][0, 4 * q : 4 * q + 4, :].bitcast(I32),
+            )
+
+        def load_words(s):
+            nc.sync.dma_start(out=w_raw[s][:], in_=word_sources[s][0].rearrange("p n i -> p (n i)").bitcast(I32))
+
+        def gather(s, i, a, b):
+            nc.vector.tensor_tensor(
+                out=picked[s][:, i, a:b],
+                in0=planes[s][i][:].indirect(lists[s][:, a // 16 : b // 16]),
+                in1=gains[s][:, a:b],
+                op=MULT,
+            )
+
+        def weave(dst, src, a, b):
+            nc.scalar.copy(
+                out=dst[:, a:b, :].rearrange("p (c u) i -> p c i u", u=4),
+                in_=src[:, :, a:b].rearrange("p i (c u) -> p c i u", u=4),
+            )
+
+        def quantize(words, scales, src, a, b):
+            nc.vector.quantize_mx(
+                out=words[:, a:b].bitcast(FP8X4),
+                scales=scales[:, a:b],
+                in_=src[:, a:b, :].rearrange("p j i -> p (j i)"),
+            )
+
+        def project(s, blk):
+            bank = psum.tile([P, PACK, BLOCK], F32, name="bank")
+            cols = slice(blk * BLOCK, (blk + 1) * BLOCK)
+            for t in range(PACK):
+                nc.tensor.matmul_mx(
+                    out=bank[:, t, :],
+                    lhsT=w_words[s][:, t, :].bitcast(FP8X4),
+                    lhsT_scale=w_scales[4 * s : P, t, :],
+                    rhs=act_words[s][:, cols].bitcast(FP8X4),
+                    rhs_scale=act_scales[s][:, cols],
+                    start=True,
+                    stop=True,
+                )
+            return bank
+
+        nc.vector.memset(ws_raw[:].bitcast(I32), 0)
+
+        nc.sync.dma_start(lists[0][:], offs)
+        nc.sync.dma_start(out=gains[0][:, 0:QUARTER], in_=wgt[:, 0:QUARTER])
+        load_plane(0, 0)
+        nc.sync.dma_start(out=gains[0][:, QUARTER:J], in_=wgt[:, QUARTER:J])
+        for i in range(1, PACK):
+            load_plane(0, i)
+            load_scale_rows(0, i - 1)
+            load_scale_rows(1, i - 1)
+        nc.sync.dma_start(lists[1][:], offs2)
+        load_scale_rows(0, 3)
+        load_scale_rows(1, 3)
+        load_words(0)
+        nc.sync.dma_start(out=gains[1][:], in_=wgt2)
+        load_plane(1, 0)
+        load_plane(1, 1)
+        load_words(1)
+        load_plane(1, 2)
+        load_plane(1, 3)
+
+        def deal_words(s):
+            nc.vector.tensor_copy(
+                out=w_words[s][:].rearrange("p t m -> p m t"),
+                in_=w_raw[s][:].rearrange("p (m t) -> p m t", t=PACK),
+            )
+
+        quarters = [(a, a + QUARTER) for a in range(0, J, QUARTER)]
+
+        gather(0, 0, 0, QUARTER)
+        gather(0, 0, QUARTER, J)
+        gather(0, 1, 0, J)
+        gather(0, 2, 0, J)
+        for a, b in quarters:
+            gather(0, 3, a, b)
+            weave(woven[0], picked[0], a, b)
+        nc.vector.tensor_copy(
+            out=w_scales[:].rearrange("p t m -> p m t"),
+            in_=ws_raw[:].rearrange("p (m t) -> p m t", t=PACK),
+        )
+        deal_words(0)
+        gather(1, 0, 0, J)
+        for a, b in quarters:
+            quantize(act_words[0], act_scales[0], woven[0], a, b)
+            for blk in range(a // BLOCK, b // BLOCK):
+                nc.scalar.copy(out=ya[:, blk, :, :], in_=project(0, blk)[:])
+        gather(1, 1, 0, J)
+        deal_words(1)
+        gather(1, 2, 0, J)
+        for a, b in quarters:
+            gather(1, 3, a, b)
+            weave(woven[1], picked[1], a, b)
+
+        out_rows = out_0.rearrange("(p t) j -> p t j", t=PACK)
+        out_words = out_1[0].rearrange("p j i -> p (j i)").bitcast(I32)
+
+        def multiply(a, b):
+            quantize(act_words[1], act_scales[1], woven[1], a, b)
+            for blk in range(a // BLOCK, b // BLOCK):
+                cols = slice(blk * BLOCK, (blk + 1) * BLOCK)
+                nc.vector.tensor_tensor(out=y[:, :, cols], in0=project(1, blk)[:], in1=ya[:, blk, :, :], op=MULT)
+            nc.sync.dma_start(out=out_rows[:, :, a:b], in_=y[:, :, a:b])
+
+        def hand_on(a, b):
+            weave(y_woven, y, a, b)
+            quantize(y_words, y_scales, y_woven, a, b)
+            nc.sync.dma_start(out=out_words[:, a:b], in_=y_words[:, a:b])
+
+        multiply(*quarters[0])
+        for n in range(1, 4):
+            multiply(*quarters[n])
+            hand_on(*quarters[n - 1])
+        hand_on(768, 896)
+        hand_on(896, 1024)
+        for q in range(4):
+            eng = nc.sync if q % 2 == 0 else nc.scalar
+            eng.dma_start(
+                out=out_2[0, 4 * q : 4 * q + 4, :].bitcast(I32),
+                in_=y_scales[32 * q : 32 * q + 4, :].bitcast(I32),
+            )

@@ -1,6 +1,7 @@
 from contextlib import ExitStack
 
 import concourse.mybir as mybir
+from concourse.masks import make_identity
 
 K, L, N, T, J = 512, 512, 512, 2048, 1024
 FLOPS = 2 * (K + L) * N * J
@@ -25,6 +26,7 @@ def tile_list_mul_noneP_kernel(
     nc = tc.nc
     with ExitStack() as ctx:
         keep = ctx.enter_context(tc.tile_pool(name="keep", bufs=1))
+        ring = ctx.enter_context(tc.tile_pool(name="ring", bufs=4))
         psum = ctx.enter_context(tc.psum_pool(name="psum", bufs=8))
 
         lists = [keep.tile([P, J // 16], U16, name="list%d" % s) for s in range(2)]
@@ -37,6 +39,9 @@ def tile_list_mul_noneP_kernel(
         w_raw = [keep.tile([P, N], I32, name="w_raw%d" % s) for s in range(2)]
         w_words = [keep.tile([P, PACK, P], I32, name="w_words%d" % s, align_bytes=64) for s in range(2)]
         ws_raw = keep.tile([P, N], U8, name="ws_raw")
+        ws_dealt = keep.tile([P, PACK, P], U8, name="ws_dealt")
+        identity = keep.tile([P, P], F32, name="identity")
+        gain_rows = keep.tile([P, P], F32, name="gain_rows")
         w_scales = keep.tile([P, PACK, P], U8, name="w_scales", align_bytes=64)
         ya = keep.tile([P, J // BLOCK, PACK, BLOCK], F32, name="ya")
         y = keep.tile([P, PACK, J], F32, name="y")
@@ -51,10 +56,10 @@ def tile_list_mul_noneP_kernel(
         def load_plane(s, i):
             nc.sync.dma_start(out=planes[s][i][:], in_=sources[s].rearrange("(p i) t -> p i t", i=PACK)[:, i, :])
 
-        def load_scale_rows(s, q):
+        def place_scale_rows(s, q):
             nc.sync.dma_start(
-                out=ws_raw[32 * q + 4 * s : 32 * q + 4 * s + 4, :].bitcast(I32),
-                in_=scale_sources[s][0, 4 * q : 4 * q + 4, :].bitcast(I32),
+                out=w_scales[32 * q + 4 * s : 32 * q + 4 * s + 4].rearrange("p t m -> p (t m)").bitcast(I32),
+                in_=ws_dealt[16 * s + 4 * q : 16 * s + 4 * q + 4].rearrange("p t m -> p (t m)").bitcast(I32),
             )
 
         def load_words(s):
@@ -82,7 +87,7 @@ def tile_list_mul_noneP_kernel(
             )
 
         def project(s, blk):
-            bank = psum.tile([P, PACK, BLOCK], F32, name="bank")
+            bank = psum.tile([P, PACK, BLOCK], F32, name="sums", tag="bank")
             cols = slice(blk * BLOCK, (blk + 1) * BLOCK)
             for t in range(PACK):
                 nc.tensor.matmul_mx(
@@ -96,21 +101,55 @@ def tile_list_mul_noneP_kernel(
                 )
             return bank
 
-        nc.vector.memset(ws_raw[:].bitcast(I32), 0)
-
-        nc.sync.dma_start(lists[0][:], offs)
-        nc.sync.dma_start(out=gains[0][:, 0:QUARTER], in_=wgt[:, 0:QUARTER])
+        gain_sources = [wgt, wgt2]
+        for s in range(2):
+            nc.sync.dma_start(
+                out=gain_rows[64 * s : 64 * s + 64, :],
+                in_=gain_sources[s][0:P:16, :].rearrange("g (b c) -> g b c", c=P),
+            )
+        for s in range(2):
+            nc.sync.dma_start(out=ws_raw[16 * s : 16 * s + 16, :].bitcast(I32), in_=scale_sources[s][0].bitcast(I32))
         load_plane(0, 0)
-        nc.sync.dma_start(out=gains[0][:, QUARTER:J], in_=wgt[:, QUARTER:J])
-        for i in range(1, PACK):
-            load_plane(0, i)
-            load_scale_rows(0, i - 1)
-            load_scale_rows(1, i - 1)
-        nc.sync.dma_start(lists[1][:], offs2)
-        load_scale_rows(0, 3)
-        load_scale_rows(1, 3)
+        nc.sync.dma_start(lists[0][:], offs)
+        load_plane(0, 1)
+        load_plane(0, 2)
+
+        make_identity(nc, identity[:])
+        nc.vector.memset(ws_raw[32:64, :].bitcast(I32), 0)
+        nc.vector.memset(ws_raw[64:P, :].bitcast(I32), 0)
+        nc.vector.memset(w_scales[:].rearrange("p t m -> p (t m)").bitcast(I32), 0)
+
+        turned = psum.tile([P, 2, 8, 8], F32, name="turned", tag="bank")
+        nc.tensor.transpose(turned[:].rearrange("c s g b -> c (s g b)"), gain_rows[:], identity[:])
+
+        def spread_gains(s, a, copy):
+            blocks = range(a // BLOCK, (a + QUARTER) // BLOCK)
+            repeated = ring.tile([P, 2, 8, 16], F32, name="repeated")
+            copy(
+                out=repeated[:],
+                in_=turned[:, s, :, blocks.start : blocks.stop].rearrange("c g b -> c b g").unsqueeze(3).to_broadcast([P, 2, 8, 16]),
+            )
+            back = psum.tile([P, 2, BLOCK], F32, name="back", tag="bank")
+            for n in range(2):
+                nc.tensor.transpose(back[:, n, :], repeated[:, n].rearrange("c g u -> c (g u)"), identity[:])
+            nc.scalar.copy(out=gains[s][:, a : a + QUARTER], in_=back[:].rearrange("p n c -> p (n c)"))
+
+        for a in range(0, J, QUARTER):
+            spread_gains(0, a, nc.vector.tensor_copy)
+        nc.vector.tensor_copy(
+            out=ws_dealt[:].rearrange("p t m -> p m t"),
+            in_=ws_raw[:].rearrange("p (m t) -> p m t", t=PACK),
+        )
+        for a in range(0, J, QUARTER):
+            spread_gains(1, a, nc.scalar.copy)
+
         load_words(0)
-        nc.sync.dma_start(out=gains[1][:], in_=wgt2)
+        for q in range(4):
+            place_scale_rows(0, q)
+        load_plane(0, 3)
+        nc.sync.dma_start(lists[1][:], offs2)
+        for q in range(4):
+            place_scale_rows(1, q)
         load_plane(1, 0)
         load_plane(1, 1)
         load_words(1)
@@ -125,18 +164,14 @@ def tile_list_mul_noneP_kernel(
 
         quarters = [(a, a + QUARTER) for a in range(0, J, QUARTER)]
 
-        gather(0, 0, 0, QUARTER)
-        gather(0, 0, QUARTER, J)
+        for a, b in quarters:
+            gather(0, 0, a, b)
         gather(0, 1, 0, J)
         gather(0, 2, 0, J)
+        deal_words(0)
         for a, b in quarters:
             gather(0, 3, a, b)
             weave(woven[0], picked[0], a, b)
-        nc.vector.tensor_copy(
-            out=w_scales[:].rearrange("p t m -> p m t"),
-            in_=ws_raw[:].rearrange("p (m t) -> p m t", t=PACK),
-        )
-        deal_words(0)
         gather(1, 0, 0, J)
         for a, b in quarters:
             quantize(act_words[0], act_scales[0], woven[0], a, b)
@@ -145,15 +180,20 @@ def tile_list_mul_noneP_kernel(
         gather(1, 1, 0, J)
         deal_words(1)
         gather(1, 2, 0, J)
-        for a, b in quarters:
+        rising = [(0, 128), (128, 256)] + quarters[1:]
+        falling = quarters[:3] + [(768, 896), (896, 1024)]
+        for n, (a, b) in enumerate(rising):
+            if n == len(rising) - 1:
+                quantize(act_words[1], act_scales[1], woven[1], *rising[0])
             gather(1, 3, a, b)
             weave(woven[1], picked[1], a, b)
+        for a, b in rising[1:]:
+            quantize(act_words[1], act_scales[1], woven[1], a, b)
 
         out_rows = out_0.rearrange("(p t) j -> p t j", t=PACK)
         out_words = out_1[0].rearrange("p j i -> p (j i)").bitcast(I32)
 
         def multiply(a, b):
-            quantize(act_words[1], act_scales[1], woven[1], a, b)
             for blk in range(a // BLOCK, b // BLOCK):
                 cols = slice(blk * BLOCK, (blk + 1) * BLOCK)
                 nc.vector.tensor_tensor(out=y[:, :, cols], in0=project(1, blk)[:], in1=ya[:, blk, :, :], op=MULT)
@@ -164,12 +204,11 @@ def tile_list_mul_noneP_kernel(
             quantize(y_words, y_scales, y_woven, a, b)
             nc.sync.dma_start(out=out_words[:, a:b], in_=y_words[:, a:b])
 
-        multiply(*quarters[0])
-        for n in range(1, 4):
-            multiply(*quarters[n])
-            hand_on(*quarters[n - 1])
-        hand_on(768, 896)
-        hand_on(896, 1024)
+        multiply(*falling[0])
+        for n in range(1, len(falling)):
+            multiply(*falling[n])
+            hand_on(*falling[n - 1])
+        hand_on(*falling[-1])
         for q in range(4):
             eng = nc.sync if q % 2 == 0 else nc.scalar
             eng.dma_start(

@@ -27,7 +27,7 @@ def tile_list_mul_noneP_kernel(
     with ExitStack() as ctx:
         keep = ctx.enter_context(tc.tile_pool(name="keep", bufs=1))
         ring = ctx.enter_context(tc.tile_pool(name="ring", bufs=4))
-        psum = ctx.enter_context(tc.psum_pool(name="psum", bufs=8))
+        psum = ctx.enter_context(tc.psum_pool(name="psum", bufs=1))
 
         lists = [keep.tile([P, J // 16], U16, name="list%d" % s) for s in range(2)]
         gains = [keep.tile([P, J], F32, name="gain%d" % s) for s in range(2)]
@@ -36,18 +36,20 @@ def tile_list_mul_noneP_kernel(
         woven = [keep.tile([P, J, PACK], BF16, name="woven%d" % s, align_bytes=64) for s in range(2)]
         act_words = [keep.tile([P, J], I32, name="act_words%d" % s, align_bytes=64) for s in range(2)]
         act_scales = [keep.tile([P, J], U8, name="act_scales%d" % s, align_bytes=64) for s in range(2)]
-        w_raw = [keep.tile([P, N], I32, name="w_raw%d" % s) for s in range(2)]
-        w_words = [keep.tile([P, PACK, P], I32, name="w_words%d" % s, align_bytes=64) for s in range(2)]
+        w_raw = keep.tile([P, 2 * N], I32, name="w_raw")
+        w_words = keep.tile([P, 2, PACK, P], I32, name="w_words", align_bytes=64)
         ws_raw = keep.tile([P, N], U8, name="ws_raw")
         ws_dealt = keep.tile([P, PACK, P], U8, name="ws_dealt")
         identity = keep.tile([P, P], F32, name="identity")
         gain_rows = keep.tile([P, P], F32, name="gain_rows")
-        w_scales = keep.tile([P, PACK, P], U8, name="w_scales", align_bytes=64)
+        w_scales = [keep.tile([P, PACK, P], U8, name="w_scales%d" % s, align_bytes=64) for s in range(2)]
         ya = keep.tile([P, J // BLOCK, PACK, BLOCK], F32, name="ya")
         y = keep.tile([P, PACK, J], F32, name="y")
         y_woven = keep.tile([P, J, PACK], BF16, name="y_woven", align_bytes=64)
         y_words = keep.tile([P, J], I32, name="y_words", align_bytes=64)
         y_scales = keep.tile([P, J], U8, name="y_scales", align_bytes=64)
+
+        banks = [psum.tile([P, 512], F32, name="bank%d" % n) for n in range(8)]
 
         sources = [xT, zT]
         scale_sources = [wa_scales, wb_scales]
@@ -58,12 +60,12 @@ def tile_list_mul_noneP_kernel(
 
         def place_scale_rows(s, q):
             nc.sync.dma_start(
-                out=w_scales[32 * q + 4 * s : 32 * q + 4 * s + 4].rearrange("p t m -> p (t m)").bitcast(I32),
+                out=w_scales[s][32 * q : 32 * q + 4].rearrange("p t m -> p (t m)").bitcast(I32),
                 in_=ws_dealt[16 * s + 4 * q : 16 * s + 4 * q + 4].rearrange("p t m -> p (t m)").bitcast(I32),
             )
 
         def load_words(s):
-            nc.sync.dma_start(out=w_raw[s][:], in_=word_sources[s][0].rearrange("p n i -> p (n i)").bitcast(I32))
+            nc.sync.dma_start(out=w_raw[:, s * N : (s + 1) * N], in_=word_sources[s][0].rearrange("p n i -> p (n i)").bitcast(I32))
 
         def gather(s, i, a, b):
             nc.vector.tensor_tensor(
@@ -73,10 +75,10 @@ def tile_list_mul_noneP_kernel(
                 op=MULT,
             )
 
-        def weave(dst, src, a, b):
+        def weave(dst, src, a, b, lo=0, hi=PACK):
             nc.scalar.copy(
-                out=dst[:, a:b, :].rearrange("p (c u) i -> p c i u", u=4),
-                in_=src[:, :, a:b].rearrange("p i (c u) -> p c i u", u=4),
+                out=dst[:, a:b, lo:hi].rearrange("p (c u) i -> p c i u", u=4),
+                in_=src[:, lo:hi, a:b].rearrange("p i (c u) -> p c i u", u=4),
             )
 
         def quantize(words, scales, src, a, b):
@@ -87,13 +89,13 @@ def tile_list_mul_noneP_kernel(
             )
 
         def project(s, blk):
-            bank = psum.tile([P, PACK, BLOCK], F32, name="sums", tag="bank")
+            bank = banks[blk][:].rearrange("p (t j) -> p t j", t=PACK)
             cols = slice(blk * BLOCK, (blk + 1) * BLOCK)
             for t in range(PACK):
                 nc.tensor.matmul_mx(
                     out=bank[:, t, :],
-                    lhsT=w_words[s][:, t, :].bitcast(FP8X4),
-                    lhsT_scale=w_scales[4 * s : P, t, :],
+                    lhsT=w_words[:, s, t, :].bitcast(FP8X4),
+                    lhsT_scale=w_scales[s][:, t, :],
                     rhs=act_words[s][:, cols].bitcast(FP8X4),
                     rhs_scale=act_scales[s][:, cols],
                     start=True,
@@ -103,12 +105,12 @@ def tile_list_mul_noneP_kernel(
 
         gain_sources = [wgt, wgt2]
         for s in range(2):
-            nc.sync.dma_start(
+            queue = (nc.sync, nc.scalar)[s]
+            queue.dma_start(out=ws_raw[16 * s : 16 * s + 16, :].bitcast(I32), in_=scale_sources[s][0].bitcast(I32))
+            queue.dma_start(
                 out=gain_rows[64 * s : 64 * s + 64, :],
                 in_=gain_sources[s][0:P:16, :].rearrange("g (b c) -> g b c", c=P),
             )
-        for s in range(2):
-            nc.sync.dma_start(out=ws_raw[16 * s : 16 * s + 16, :].bitcast(I32), in_=scale_sources[s][0].bitcast(I32))
         load_plane(0, 0)
         nc.sync.dma_start(lists[0][:], offs)
         load_plane(0, 1)
@@ -117,98 +119,107 @@ def tile_list_mul_noneP_kernel(
         make_identity(nc, identity[:])
         nc.vector.memset(ws_raw[32:64, :].bitcast(I32), 0)
         nc.vector.memset(ws_raw[64:P, :].bitcast(I32), 0)
-        nc.vector.memset(w_scales[:].rearrange("p t m -> p (t m)").bitcast(I32), 0)
+        for s in range(2):
+            nc.vector.memset(w_scales[s][:].rearrange("p t m -> p (t m)").bitcast(I32), 0)
 
-        turned = psum.tile([P, 2, 8, 8], F32, name="turned", tag="bank")
-        nc.tensor.transpose(turned[:].rearrange("c s g b -> c (s g b)"), gain_rows[:], identity[:])
-
-        def spread_gains(s, a, copy):
-            blocks = range(a // BLOCK, (a + QUARTER) // BLOCK)
-            repeated = ring.tile([P, 2, 8, 16], F32, name="repeated")
-            copy(
-                out=repeated[:],
-                in_=turned[:, s, :, blocks.start : blocks.stop].rearrange("c g b -> c b g").unsqueeze(3).to_broadcast([P, 2, 8, 16]),
-            )
-            back = psum.tile([P, 2, BLOCK], F32, name="back", tag="bank")
-            for n in range(2):
-                nc.tensor.transpose(back[:, n, :], repeated[:, n].rearrange("c g u -> c (g u)"), identity[:])
-            nc.scalar.copy(out=gains[s][:, a : a + QUARTER], in_=back[:].rearrange("p n c -> p (n c)"))
-
-        for a in range(0, J, QUARTER):
-            spread_gains(0, a, nc.vector.tensor_copy)
         nc.vector.tensor_copy(
             out=ws_dealt[:].rearrange("p t m -> p m t"),
             in_=ws_raw[:].rearrange("p (m t) -> p m t", t=PACK),
         )
-        for a in range(0, J, QUARTER):
-            spread_gains(1, a, nc.scalar.copy)
+        def spread_gains(s, turn_bank, back_banks, copy):
+            nc.tensor.transpose(banks[turn_bank][:, 0:P], gain_rows[:], identity[:])
+            turned = banks[turn_bank][:, 64 * s : 64 * s + 64].rearrange("c (g b) -> c b g", b=8)
+            for q in range(4):
+                repeated = ring.tile([P, 2, 8, 16], F32, name="repeated")
+                copy(out=repeated[:], in_=turned[:, 2 * q : 2 * q + 2, :].unsqueeze(3).to_broadcast([P, 2, 8, 16]))
+                back = banks[back_banks[q]]
+                for n in range(2):
+                    nc.tensor.transpose(back[:, n * P : (n + 1) * P], repeated[:, n].rearrange("c g u -> c (g u)"), identity[:])
+                nc.scalar.copy(out=gains[s][:, q * QUARTER : (q + 1) * QUARTER], in_=back[:, 0:QUARTER])
 
-        load_words(0)
-        for q in range(4):
-            place_scale_rows(0, q)
+        spread_gains(0, 0, [1, 2, 3, 4], nc.vector.tensor_copy)
+        spread_gains(1, 4, [5, 6, 7, 1], nc.scalar.copy)
+
+        place_scale_rows(0, 0)
+        place_scale_rows(0, 1)
         load_plane(0, 3)
-        nc.sync.dma_start(lists[1][:], offs2)
-        for q in range(4):
-            place_scale_rows(1, q)
-        load_plane(1, 0)
-        load_plane(1, 1)
+        place_scale_rows(0, 2)
+        place_scale_rows(0, 3)
+        load_words(0)
         load_words(1)
+        nc.sync.dma_start(lists[1][:], offs2)
+        load_plane(1, 0)
+        place_scale_rows(1, 0)
+        load_plane(1, 1)
+        place_scale_rows(1, 1)
+        place_scale_rows(1, 2)
         load_plane(1, 2)
+        place_scale_rows(1, 3)
         load_plane(1, 3)
 
-        def deal_words(s):
+        def deal_words():
             nc.vector.tensor_copy(
-                out=w_words[s][:].rearrange("p t m -> p m t"),
-                in_=w_raw[s][:].rearrange("p (m t) -> p m t", t=PACK),
+                out=w_words[:].rearrange("p s t m -> p s m t"),
+                in_=w_raw[:].rearrange("p (s m t) -> p s m t", s=2, t=PACK),
             )
 
         quarters = [(a, a + QUARTER) for a in range(0, J, QUARTER)]
 
-        for a, b in quarters:
+        halves = [(0, 512), (512, J)]
+        for a, b in quarters[:2] + halves[1:]:
             gather(0, 0, a, b)
         gather(0, 1, 0, J)
+        for a, b in halves:
+            weave(woven[0], picked[0], a, b, 0, 2)
         gather(0, 2, 0, J)
-        deal_words(0)
-        for a, b in quarters:
+        for a, b in halves:
             gather(0, 3, a, b)
-            weave(woven[0], picked[0], a, b)
+            weave(woven[0], picked[0], a, b, 2, 4)
+        deal_words()
         gather(1, 0, 0, J)
-        for a, b in quarters:
+        for a, b in halves:
             quantize(act_words[0], act_scales[0], woven[0], a, b)
             for blk in range(a // BLOCK, b // BLOCK):
-                nc.scalar.copy(out=ya[:, blk, :, :], in_=project(0, blk)[:])
+                nc.scalar.copy(out=ya[:, blk, :, :], in_=project(0, blk))
         gather(1, 1, 0, J)
-        deal_words(1)
+        for a, b in halves:
+            weave(woven[1], picked[1], a, b, 0, 2)
         gather(1, 2, 0, J)
-        rising = [(0, 128), (128, 256)] + quarters[1:]
-        falling = quarters[:3] + [(768, 896), (896, 1024)]
-        for n, (a, b) in enumerate(rising):
-            if n == len(rising) - 1:
-                quantize(act_words[1], act_scales[1], woven[1], *rising[0])
-            gather(1, 3, a, b)
-            weave(woven[1], picked[1], a, b)
-        for a, b in rising[1:]:
-            quantize(act_words[1], act_scales[1], woven[1], a, b)
 
         out_rows = out_0.rearrange("(p t) j -> p t j", t=PACK)
         out_words = out_1[0].rearrange("p j i -> p (j i)").bitcast(I32)
+        weave_from = {256: 0, 512: 256, 640: 512, 768: 640, 896: 768, 1024: 896}
+        store_from = {256: 0, 512: 256, 768: 512, 896: 768, 1024: 896}
 
-        def multiply(a, b):
-            for blk in range(a // BLOCK, b // BLOCK):
-                cols = slice(blk * BLOCK, (blk + 1) * BLOCK)
-                nc.vector.tensor_tensor(out=y[:, :, cols], in0=project(1, blk)[:], in1=ya[:, blk, :, :], op=MULT)
-            nc.sync.dma_start(out=out_rows[:, :, a:b], in_=y[:, :, a:b])
+        def multiply(blk):
+            a, b = blk * BLOCK, (blk + 1) * BLOCK
+            nc.vector.tensor_tensor(out=y[:, :, a:b], in0=project(1, blk), in1=ya[:, blk, :, :], op=MULT)
+            if b in store_from:
+                nc.sync.dma_start(out=out_rows[:, :, store_from[b] : b], in_=y[:, :, store_from[b] : b])
+            if b in weave_from:
+                weave(y_woven, y, weave_from[b], b)
 
-        def hand_on(a, b):
-            weave(y_woven, y, a, b)
+        def hand_on(a, b, first=None):
             quantize(y_words, y_scales, y_woven, a, b)
-            nc.sync.dma_start(out=out_words[:, a:b], in_=y_words[:, a:b])
+            if first is not None:
+                nc.sync.dma_start(out=out_words[:, first:b], in_=y_words[:, first:b])
 
-        multiply(*falling[0])
-        for n in range(1, len(falling)):
-            multiply(*falling[n])
-            hand_on(*falling[n - 1])
-        hand_on(*falling[-1])
+        for a, b in quarters:
+            gather(1, 3, a, b)
+            weave(woven[1], picked[1], a, b, 2, 4)
+        for n, (a, b) in enumerate(quarters):
+            quantize(act_words[1], act_scales[1], woven[1], a, b)
+            if n > 0:
+                multiply(n - 1)
+        multiply(3)
+        multiply(4)
+        multiply(5)
+        hand_on(0, 512, 0)
+        multiply(6)
+        multiply(7)
+        hand_on(512, 768)
+        hand_on(768, 896, 512)
+        hand_on(896, 1024, 896)
         for q in range(4):
             eng = nc.sync if q % 2 == 0 else nc.scalar
             eng.dma_start(

@@ -43,7 +43,7 @@ def tile_list_mul_noneP_kernel(
         identity = keep.tile([P, P], F32, name="identity")
         gain_rows = keep.tile([P, P], F32, name="gain_rows")
         w_scales = [keep.tile([P, PACK, P], U8, name="w_scales%d" % s, align_bytes=64) for s in range(2)]
-        ya = keep.tile([P, J // BLOCK, PACK, BLOCK], F32, name="ya")
+        ya = keep.tile([P, 8, 512], F32, name="ya")
         y = keep.tile([P, PACK, J], F32, name="y")
         y_woven = keep.tile([P, J, PACK], BF16, name="y_woven", align_bytes=64)
         y_words = keep.tile([P, J], I32, name="y_words", align_bytes=64)
@@ -88,28 +88,28 @@ def tile_list_mul_noneP_kernel(
                 in_=src[:, a:b, :].rearrange("p j i -> p (j i)"),
             )
 
-        def project(s, blk):
-            bank = banks[blk][:].rearrange("p (t j) -> p t j", t=PACK)
-            cols = slice(blk * BLOCK, (blk + 1) * BLOCK)
-            for t in range(PACK):
+        units = [(0, 4, 0, 128), (0, 4, 128, 256)]
+        units = units + [(t, t + 2, a, a + QUARTER) for a in (256, 512) for t in (0, 2)]
+        units = units + [(0, 4, 768, 896), (0, 4, 896, 1024)]
+
+        def project(s, n):
+            t0, t1, a, b = units[n]
+            for t in range(t0, t1):
                 nc.tensor.matmul_mx(
-                    out=bank[:, t, :],
+                    out=banks[n][:, (t - t0) * (b - a) : (t - t0 + 1) * (b - a)],
                     lhsT=w_words[:, s, t, :].bitcast(FP8X4),
                     lhsT_scale=w_scales[s][:, t, :],
-                    rhs=act_words[s][:, cols].bitcast(FP8X4),
-                    rhs_scale=act_scales[s][:, cols],
+                    rhs=act_words[s][:, a:b].bitcast(FP8X4),
+                    rhs_scale=act_scales[s][:, a:b],
                     start=True,
                     stop=True,
                 )
-            return bank
+            return banks[n][:]
 
-        gain_sources = [wgt, wgt2]
+        nc.sync.dma_start(out=gain_rows[0:64, :], in_=wgt[0:P:16, :].rearrange("g (b c) -> g b c", c=P))
         for s in range(2):
-            queue = (nc.sync, nc.scalar)[s]
-            queue.dma_start(out=ws_raw[16 * s : 16 * s + 16, :].bitcast(I32), in_=scale_sources[s][0].bitcast(I32))
-            queue.dma_start(
-                out=gain_rows[64 * s : 64 * s + 64, :],
-                in_=gain_sources[s][0:P:16, :].rearrange("g (b c) -> g b c", c=P),
+            (nc.sync, nc.scalar)[s].dma_start(
+                out=ws_raw[16 * s : 16 * s + 16, :].bitcast(I32), in_=scale_sources[s][0].bitcast(I32)
             )
         load_plane(0, 0)
         nc.sync.dma_start(lists[0][:], offs)
@@ -117,14 +117,15 @@ def tile_list_mul_noneP_kernel(
         load_plane(0, 2)
 
         make_identity(nc, identity[:])
+        nc.vector.memset(gain_rows[64:P, :], 0.0)
         nc.vector.memset(ws_raw[32:64, :].bitcast(I32), 0)
         nc.vector.memset(ws_raw[64:P, :].bitcast(I32), 0)
         for s in range(2):
             nc.vector.memset(w_scales[s][:].rearrange("p t m -> p (t m)").bitcast(I32), 0)
 
         nc.vector.tensor_copy(
-            out=ws_dealt[:].rearrange("p t m -> p m t"),
-            in_=ws_raw[:].rearrange("p (m t) -> p m t", t=PACK),
+            out=ws_dealt[:],
+            in_=ws_raw[:].rearrange("p (m t) -> p t m", t=PACK),
         )
         def spread_gains(s, turn_bank, back_banks, copy):
             nc.tensor.transpose(banks[turn_bank][:, 0:P], gain_rows[:], identity[:])
@@ -138,7 +139,6 @@ def tile_list_mul_noneP_kernel(
                 nc.scalar.copy(out=gains[s][:, q * QUARTER : (q + 1) * QUARTER], in_=back[:, 0:QUARTER])
 
         spread_gains(0, 0, [1, 2, 3, 4], nc.vector.tensor_copy)
-        spread_gains(1, 4, [5, 6, 7, 1], nc.scalar.copy)
 
         place_scale_rows(0, 0)
         place_scale_rows(0, 1)
@@ -148,6 +148,7 @@ def tile_list_mul_noneP_kernel(
         load_words(0)
         load_words(1)
         nc.sync.dma_start(lists[1][:], offs2)
+        nc.sync.dma_start(out=gains[1][:], in_=wgt2)
         load_plane(1, 0)
         place_scale_rows(1, 0)
         load_plane(1, 1)
@@ -159,8 +160,8 @@ def tile_list_mul_noneP_kernel(
 
         def deal_words():
             nc.vector.tensor_copy(
-                out=w_words[:].rearrange("p s t m -> p s m t"),
-                in_=w_raw[:].rearrange("p (s m t) -> p s m t", s=2, t=PACK),
+                out=w_words[:].rearrange("p s t (c u) -> p s c t u", u=4),
+                in_=w_raw[:].rearrange("p (s c u t) -> p s c t u", s=2, u=4, t=PACK),
             )
 
         quarters = [(a, a + QUARTER) for a in range(0, J, QUARTER)]
@@ -168,19 +169,19 @@ def tile_list_mul_noneP_kernel(
         halves = [(0, 512), (512, J)]
         for a, b in quarters[:2] + halves[1:]:
             gather(0, 0, a, b)
-        gather(0, 1, 0, J)
         for a, b in halves:
+            gather(0, 1, a, b)
             weave(woven[0], picked[0], a, b, 0, 2)
         gather(0, 2, 0, J)
-        for a, b in halves:
+        for a, b in quarters:
             gather(0, 3, a, b)
             weave(woven[0], picked[0], a, b, 2, 4)
         deal_words()
-        gather(1, 0, 0, J)
         for a, b in halves:
             quantize(act_words[0], act_scales[0], woven[0], a, b)
             for blk in range(a // BLOCK, b // BLOCK):
-                nc.scalar.copy(out=ya[:, blk, :, :], in_=project(0, blk))
+                nc.scalar.copy(out=ya[:, blk, :], in_=project(0, blk))
+        gather(1, 0, 0, J)
         gather(1, 1, 0, J)
         for a, b in halves:
             weave(woven[1], picked[1], a, b, 0, 2)
@@ -188,35 +189,54 @@ def tile_list_mul_noneP_kernel(
 
         out_rows = out_0.rearrange("(p t) j -> p t j", t=PACK)
         out_words = out_1[0].rearrange("p j i -> p (j i)").bitcast(I32)
-        weave_from = {256: 0, 512: 256, 640: 512, 768: 640, 896: 768, 1024: 896}
-        store_from = {256: 0, 512: 256, 768: 512, 896: 768, 1024: 896}
-
-        def multiply(blk):
-            a, b = blk * BLOCK, (blk + 1) * BLOCK
-            nc.vector.tensor_tensor(out=y[:, :, a:b], in0=project(1, blk), in1=ya[:, blk, :, :], op=MULT)
-            if b in store_from:
-                nc.sync.dma_start(out=out_rows[:, :, store_from[b] : b], in_=y[:, :, store_from[b] : b])
-            if b in weave_from:
-                weave(y_woven, y, weave_from[b], b)
+        def multiply(n):
+            t0, t1, a, b = units[n]
+            nc.vector.tensor_tensor(
+                out=y[:, t0:t1, a:b],
+                in0=project(1, n).rearrange("p (t j) -> p t j", j=b - a),
+                in1=ya[:, n, :].rearrange("p (t j) -> p t j", j=b - a),
+                op=MULT,
+            )
+            nc.sync.dma_start(out=out_rows[:, t0:t1, a:b], in_=y[:, t0:t1, a:b])
 
         def hand_on(a, b, first=None):
             quantize(y_words, y_scales, y_woven, a, b)
             if first is not None:
                 nc.sync.dma_start(out=out_words[:, first:b], in_=y_words[:, first:b])
 
-        for a, b in quarters:
-            gather(1, 3, a, b)
-            weave(woven[1], picked[1], a, b, 2, 4)
-        for n, (a, b) in enumerate(quarters):
-            quantize(act_words[1], act_scales[1], woven[1], a, b)
-            if n > 0:
-                multiply(n - 1)
+        rising = [(0, 128), (128, 256)] + quarters[1:]
+
+        def last_gather(n):
+            gather(1, 3, *rising[n])
+            weave(woven[1], picked[1], *rising[n], 2, 4)
+
+        def quantize_z(n):
+            quantize(act_words[1], act_scales[1], woven[1], *rising[n])
+
+        last_gather(0)
+        last_gather(1)
+        last_gather(2)
+        quantize_z(0)
+        last_gather(3)
+        quantize_z(1)
+        last_gather(4)
+        multiply(0)
+        quantize_z(2)
+        multiply(1)
+        weave(y_woven, y, 0, 256)
+        quantize_z(3)
+        multiply(2)
+        quantize_z(4)
         multiply(3)
+        weave(y_woven, y, 256, 512)
         multiply(4)
         multiply(5)
+        weave(y_woven, y, 512, 768)
         hand_on(0, 512, 0)
         multiply(6)
+        weave(y_woven, y, 768, 896)
         multiply(7)
+        weave(y_woven, y, 896, 1024)
         hand_on(512, 768)
         hand_on(768, 896, 512)
         hand_on(896, 1024, 896)

@@ -41,7 +41,7 @@ def tile_list_mul_noneP_kernel(
         ws_raw = keep.tile([P, N], U8, name="ws_raw")
         ws_dealt = keep.tile([P, PACK, P], U8, name="ws_dealt")
         identity = keep.tile([P, P], F32, name="identity")
-        gain_rows = keep.tile([P, P], F32, name="gain_rows")
+        gain_rows = [keep.tile([P, P], F32, name="gain_rows%d" % s) for s in range(2)]
         w_scales = [keep.tile([P, PACK, P], U8, name="w_scales%d" % s, align_bytes=64) for s in range(2)]
         ya = keep.tile([P, 8, 512], F32, name="ya")
         y = keep.tile([P, PACK, J], F32, name="y")
@@ -106,18 +106,23 @@ def tile_list_mul_noneP_kernel(
                 )
             return banks[n][:]
 
-        nc.sync.dma_start(out=gain_rows[0:64, :], in_=wgt[0:P:16, :].rearrange("g (b c) -> g b c", c=P))
+        def load_gain_rows(s):
+            nc.sync.dma_start(out=gain_rows[s][0:64, :], in_=(wgt, wgt2)[s][0:P:16, :].rearrange("g (b c) -> g b c", c=P))
+
+        load_gain_rows(0)
         for s in range(2):
             (nc.sync, nc.scalar)[s].dma_start(
                 out=ws_raw[16 * s : 16 * s + 16, :].bitcast(I32), in_=scale_sources[s][0].bitcast(I32)
             )
         load_plane(0, 0)
         nc.sync.dma_start(lists[0][:], offs)
+        load_gain_rows(1)
         load_plane(0, 1)
         load_plane(0, 2)
 
         make_identity(nc, identity[:])
-        nc.vector.memset(gain_rows[64:P, :], 0.0)
+        for s in range(2):
+            nc.vector.memset(gain_rows[s][64:P, :], 0.0)
         nc.vector.memset(ws_raw[32:64, :].bitcast(I32), 0)
         nc.vector.memset(ws_raw[64:P, :].bitcast(I32), 0)
         for s in range(2):
@@ -128,8 +133,8 @@ def tile_list_mul_noneP_kernel(
             in_=ws_raw[:].rearrange("p (m t) -> p t m", t=PACK),
         )
         def spread_gains(s, turn_bank, back_banks, copy):
-            nc.tensor.transpose(banks[turn_bank][:, 0:P], gain_rows[:], identity[:])
-            turned = banks[turn_bank][:, 64 * s : 64 * s + 64].rearrange("c (g b) -> c b g", b=8)
+            nc.tensor.transpose(banks[turn_bank][:, 0:P], gain_rows[s][:], identity[:])
+            turned = banks[turn_bank][:, 0:64].rearrange("c (g b) -> c b g", b=8)
             for q in range(4):
                 repeated = ring.tile([P, 2, 8, 16], F32, name="repeated")
                 copy(out=repeated[:], in_=turned[:, 2 * q : 2 * q + 2, :].unsqueeze(3).to_broadcast([P, 2, 8, 16]))
@@ -139,6 +144,7 @@ def tile_list_mul_noneP_kernel(
                 nc.scalar.copy(out=gains[s][:, q * QUARTER : (q + 1) * QUARTER], in_=back[:, 0:QUARTER])
 
         spread_gains(0, 0, [1, 2, 3, 4], nc.vector.tensor_copy)
+        spread_gains(1, 4, [5, 6, 7, 1], nc.scalar.copy)
 
         place_scale_rows(0, 0)
         place_scale_rows(0, 1)
@@ -148,7 +154,6 @@ def tile_list_mul_noneP_kernel(
         load_words(0)
         load_words(1)
         nc.sync.dma_start(lists[1][:], offs2)
-        nc.sync.dma_start(out=gains[1][:], in_=wgt2)
         load_plane(1, 0)
         place_scale_rows(1, 0)
         load_plane(1, 1)
@@ -177,13 +182,13 @@ def tile_list_mul_noneP_kernel(
             gather(0, 3, a, b)
             weave(woven[0], picked[0], a, b, 2, 4)
         deal_words()
-        for a, b in halves:
+        for a, b in halves[:1] + quarters[2:]:
             quantize(act_words[0], act_scales[0], woven[0], a, b)
             for blk in range(a // BLOCK, b // BLOCK):
                 nc.scalar.copy(out=ya[:, blk, :], in_=project(0, blk))
         gather(1, 0, 0, J)
-        gather(1, 1, 0, J)
         for a, b in halves:
+            gather(1, 1, a, b)
             weave(woven[1], picked[1], a, b, 0, 2)
         gather(1, 2, 0, J)
 

from contextlib import ExitStack

import concourse.mybir as mybir
from concourse.masks import make_identity

K, L, N, T, J = 512, 512, 512, 2048, 1024
FLOPS = 2 * (K + L) * N * J

F32 = mybir.dt.float32
BF16 = mybir.dt.bfloat16
I32 = mybir.dt.int32
U16 = mybir.dt.uint16
U8 = mybir.dt.uint8
FP8X4 = mybir.dt.float8_e4m3fn_x4
MULT = mybir.AluOpType.mult

P = 128
PACK = 4
BLOCK = 128
QUARTER = 256


def tile_list_mul_noneP_kernel(
    tc, xT, wgt, zT, wgt2, wa_words, wa_scales, wb_words, wb_scales, offs, offs2, out_0, out_1, out_2
):
    nc = tc.nc
    with ExitStack() as ctx:
        keep = ctx.enter_context(tc.tile_pool(name="keep", bufs=1))
        ring = ctx.enter_context(tc.tile_pool(name="ring", bufs=4))
        psum = ctx.enter_context(tc.psum_pool(name="psum", bufs=1))

        lists = [keep.tile([P, J // 16], U16, name="list%d" % s) for s in range(2)]
        gains = [keep.tile([P, J], F32, name="gain%d" % s) for s in range(2)]
        planes = [[keep.tile([P, T], F32, name="plane%d_%d" % (s, i)) for i in range(PACK)] for s in range(2)]
        picked = [keep.tile([P, PACK, J], F32, name="picked%d" % s) for s in range(2)]
        woven = [keep.tile([P, J, PACK], BF16, name="woven%d" % s, align_bytes=64) for s in range(2)]
        act_words = [keep.tile([P, J], I32, name="act_words%d" % s, align_bytes=64) for s in range(2)]
        act_scales = [keep.tile([P, J], U8, name="act_scales%d" % s, align_bytes=64) for s in range(2)]
        w_raw = keep.tile([P, 2 * N], I32, name="w_raw")
        w_words = keep.tile([P, 2, PACK, P], I32, name="w_words", align_bytes=64)
        ws_raw = keep.tile([P, N], U8, name="ws_raw")
        ws_dealt = keep.tile([P, PACK, P], U8, name="ws_dealt")
        identity = keep.tile([P, P], F32, name="identity")
        gain_rows = [keep.tile([P, P], F32, name="gain_rows%d" % s) for s in range(2)]
        w_scales = [keep.tile([P, PACK, P], U8, name="w_scales%d" % s, align_bytes=64) for s in range(2)]
        ya = keep.tile([P, 8, 512], F32, name="ya")
        y = keep.tile([P, PACK, J], F32, name="y")
        y_woven = keep.tile([P, J, PACK], BF16, name="y_woven", align_bytes=64)
        y_words = keep.tile([P, J], I32, name="y_words", align_bytes=64)
        y_scales = keep.tile([P, J], U8, name="y_scales", align_bytes=64)

        banks = [psum.tile([P, 512], F32, name="bank%d" % n) for n in range(8)]

        sources = [xT, zT]
        scale_sources = [wa_scales, wb_scales]
        word_sources = [wa_words, wb_words]

        def load_plane(s, i):
            nc.sync.dma_start(out=planes[s][i][:], in_=sources[s].rearrange("(p i) t -> p i t", i=PACK)[:, i, :])

        def place_scale_rows(s, q):
            nc.sync.dma_start(
                out=w_scales[s][32 * q : 32 * q + 4].rearrange("p t m -> p (t m)").bitcast(I32),
                in_=ws_dealt[16 * s + 4 * q : 16 * s + 4 * q + 4].rearrange("p t m -> p (t m)").bitcast(I32),
            )

        def load_words(s):
            nc.sync.dma_start(out=w_raw[:, s * N : (s + 1) * N], in_=word_sources[s][0].rearrange("p n i -> p (n i)").bitcast(I32))

        def gather(s, i, a, b):
            nc.vector.tensor_tensor(
                out=picked[s][:, i, a:b],
                in0=planes[s][i][:].indirect(lists[s][:, a // 16 : b // 16]),
                in1=gains[s][:, a:b],
                op=MULT,
            )

        def weave(dst, src, a, b, lo=0, hi=PACK):
            nc.scalar.copy(
                out=dst[:, a:b, lo:hi].rearrange("p (c u) i -> p c i u", u=4),
                in_=src[:, lo:hi, a:b].rearrange("p i (c u) -> p c i u", u=4),
            )

        def quantize(words, scales, src, a, b):
            nc.vector.quantize_mx(
                out=words[:, a:b].bitcast(FP8X4),
                scales=scales[:, a:b],
                in_=src[:, a:b, :].rearrange("p j i -> p (j i)"),
            )

        units = [(0, 4, 0, 128), (0, 4, 128, 256)]
        units = units + [(t, t + 2, a, a + QUARTER) for a in (256, 512) for t in (0, 2)]
        units = units + [(0, 4, 768, 896), (0, 4, 896, 1024)]

        def project(s, n):
            t0, t1, a, b = units[n]
            for t in range(t0, t1):
                nc.tensor.matmul_mx(
                    out=banks[n][:, (t - t0) * (b - a) : (t - t0 + 1) * (b - a)],
                    lhsT=w_words[:, s, t, :].bitcast(FP8X4),
                    lhsT_scale=w_scales[s][:, t, :],
                    rhs=act_words[s][:, a:b].bitcast(FP8X4),
                    rhs_scale=act_scales[s][:, a:b],
                    start=True,
                    stop=True,
                )
            return banks[n][:]

        def load_gain_rows(s):
            nc.sync.dma_start(out=gain_rows[s][0:64, :], in_=(wgt, wgt2)[s][0:P:16, :].rearrange("g (b c) -> g b c", c=P))

        load_gain_rows(0)
        for s in range(2):
            (nc.sync, nc.scalar)[s].dma_start(
                out=ws_raw[16 * s : 16 * s + 16, :].bitcast(I32), in_=scale_sources[s][0].bitcast(I32)
            )
        load_plane(0, 0)
        nc.sync.dma_start(lists[0][:], offs)
        load_gain_rows(1)
        load_plane(0, 1)
        load_plane(0, 2)

        make_identity(nc, identity[:])
        for s in range(2):
            nc.vector.memset(gain_rows[s][64:P, :], 0.0)
        nc.vector.memset(ws_raw[32:64, :].bitcast(I32), 0)
        nc.vector.memset(ws_raw[64:P, :].bitcast(I32), 0)
        for s in range(2):
            nc.vector.memset(w_scales[s][:].rearrange("p t m -> p (t m)").bitcast(I32), 0)

        nc.vector.tensor_copy(
            out=ws_dealt[:],
            in_=ws_raw[:].rearrange("p (m t) -> p t m", t=PACK),
        )
        def spread_gains(s, turn_bank, back_banks, copy):
            nc.tensor.transpose(banks[turn_bank][:, 0:P], gain_rows[s][:], identity[:])
            turned = banks[turn_bank][:, 0:64].rearrange("c (g b) -> c b g", b=8)
            for q in range(4):
                repeated = ring.tile([P, 2, 8, 16], F32, name="repeated")
                copy(out=repeated[:], in_=turned[:, 2 * q : 2 * q + 2, :].unsqueeze(3).to_broadcast([P, 2, 8, 16]))
                back = banks[back_banks[q]]
                for n in range(2):
                    nc.tensor.transpose(back[:, n * P : (n + 1) * P], repeated[:, n].rearrange("c g u -> c (g u)"), identity[:])
                nc.scalar.copy(out=gains[s][:, q * QUARTER : (q + 1) * QUARTER], in_=back[:, 0:QUARTER])

        spread_gains(0, 0, [1, 2, 3, 4], nc.vector.tensor_copy)
        spread_gains(1, 4, [5, 6, 7, 1], nc.scalar.copy)

        place_scale_rows(0, 0)
        place_scale_rows(0, 1)
        load_plane(0, 3)
        place_scale_rows(0, 2)
        place_scale_rows(0, 3)
        load_words(0)
        load_words(1)
        nc.sync.dma_start(lists[1][:], offs2)
        load_plane(1, 0)
        place_scale_rows(1, 0)
        load_plane(1, 1)
        place_scale_rows(1, 1)
        place_scale_rows(1, 2)
        load_plane(1, 2)
        place_scale_rows(1, 3)
        load_plane(1, 3)

        def deal_words():
            nc.vector.tensor_copy(
                out=w_words[:].rearrange("p s t (c u) -> p s c t u", u=4),
                in_=w_raw[:].rearrange("p (s c u t) -> p s c t u", s=2, u=4, t=PACK),
            )

        quarters = [(a, a + QUARTER) for a in range(0, J, QUARTER)]

        halves = [(0, 512), (512, J)]
        for a, b in quarters[:2] + halves[1:]:
            gather(0, 0, a, b)
        for a, b in halves:
            gather(0, 1, a, b)
            weave(woven[0], picked[0], a, b, 0, 2)
        gather(0, 2, 0, J)
        for a, b in quarters:
            gather(0, 3, a, b)
            weave(woven[0], picked[0], a, b, 2, 4)
        deal_words()
        for a, b in halves[:1] + quarters[2:]:
            quantize(act_words[0], act_scales[0], woven[0], a, b)
            for blk in range(a // BLOCK, b // BLOCK):
                nc.scalar.copy(out=ya[:, blk, :], in_=project(0, blk))
        gather(1, 0, 0, J)
        for a, b in halves:
            gather(1, 1, a, b)
            weave(woven[1], picked[1], a, b, 0, 2)
        gather(1, 2, 0, J)

        out_rows = out_0.rearrange("(p t) j -> p t j", t=PACK)
        out_words = out_1[0].rearrange("p j i -> p (j i)").bitcast(I32)
        def multiply(n):
            t0, t1, a, b = units[n]
            nc.vector.tensor_tensor(
                out=y[:, t0:t1, a:b],
                in0=project(1, n).rearrange("p (t j) -> p t j", j=b - a),
                in1=ya[:, n, :].rearrange("p (t j) -> p t j", j=b - a),
                op=MULT,
            )
            nc.sync.dma_start(out=out_rows[:, t0:t1, a:b], in_=y[:, t0:t1, a:b])

        def hand_on(a, b, first=None):
            quantize(y_words, y_scales, y_woven, a, b)
            if first is not None:
                nc.sync.dma_start(out=out_words[:, first:b], in_=y_words[:, first:b])

        rising = [(0, 128), (128, 256)] + quarters[1:]

        def last_gather(n):
            gather(1, 3, *rising[n])
            weave(woven[1], picked[1], *rising[n], 2, 4)

        def quantize_z(n):
            quantize(act_words[1], act_scales[1], woven[1], *rising[n])

        last_gather(0)
        last_gather(1)
        last_gather(2)
        quantize_z(0)
        last_gather(3)
        quantize_z(1)
        last_gather(4)
        multiply(0)
        quantize_z(2)
        multiply(1)
        weave(y_woven, y, 0, 256)
        quantize_z(3)
        multiply(2)
        quantize_z(4)
        multiply(3)
        weave(y_woven, y, 256, 512)
        multiply(4)
        multiply(5)
        weave(y_woven, y, 512, 768)
        hand_on(0, 512, 0)
        multiply(6)
        weave(y_woven, y, 768, 896)
        multiply(7)
        weave(y_woven, y, 896, 1024)
        hand_on(512, 768)
        hand_on(768, 896, 512)
        hand_on(896, 1024, 896)
        for q in range(4):
            eng = nc.sync if q % 2 == 0 else nc.scalar
            eng.dma_start(
                out=out_2[0, 4 * q : 4 * q + 4, :].bitcast(I32),
                in_=y_scales[32 * q : 32 * q + 4, :].bitcast(I32),
            )
